import numpy as np, ml_dtypes
CORES = [14,30,46,142,158,174,270,286,302,398,414,430]
N = 12
W = 64
def setup_inputs(rng):
    return {"x": rng.standard_normal((N, 128, W), dtype=np.float32).astype(ml_dtypes.bfloat16), "a": (7 + rng.standard_normal((N, 128, W), dtype=np.float32) - 9 * (rng.random((N, 128, W)) < 2.0 / (N * W))).astype(ml_dtypes.bfloat16)}
def setup_inputs_big(rng):
    d = setup_inputs(rng)
    for k in ("x",): d[k] = (d[k].astype(np.float32) * 1048576.0).astype(d[k].dtype)
    return d
def setup_inputs_small(rng):
    d = setup_inputs(rng)
    for k in ("x",): d[k] = (d[k].astype(np.float32) * (1 / 1048576.0)).astype(d[k].dtype)
    return d
def setup_inputs_apart(rng):
    d = setup_inputs(rng)
    f = (10.0 ** rng.permutation(np.linspace(-1.5, 1.5, N))).astype(np.float32).reshape(N, 1, 1)
    for k in ("x",): d[k] = (d[k].astype(np.float32) * f).astype(d[k].dtype)
    return d
def reference(x, a):
    X = np.concatenate(list(x.astype(np.float64)), axis=1); G = 1.0 / (1.0 + np.exp(-np.concatenate(list(a.astype(np.float64)), axis=1)))
    h = np.zeros(128); H = np.zeros_like(X)
    for c in range(N * W):
        h = G[:, c] * h + X[:, c]; H[:, c] = h
    return {"y": np.stack([H[:, W * r:W * r + W] for r in range(N)]).astype(ml_dtypes.bfloat16)}

@@ -1,0 +1,181 @@
+from concourse.bass import DstId, RemoteDMATransfer
+from concourse.mybir import AluOpType, AxisListType, ActivationFunctionType
+
+W = 64
+PAD = 8
+SL = PAD + W
+GROUP = 6
+NE = 8
+
+SCRATCH = {
+    "ab": ("sbuf", [128, W], "bfloat16"),
+    "xe": ("sbuf", [128, SL], "bfloat16"),
+    "ge": ("sbuf", [128, SL], "float32"),
+    "buf": ("sbuf", [128, GROUP * SL], "float32"),
+    "cs": ("sbuf", [128, 8], "float32"),
+    "cl": ("sbuf", [128, 4], "float32"),
+    "yb": ("sbuf", [128, SL], "bfloat16"),
+}
+SEMAPHORES = ["lda", "ldx", "go", "sg", "sm", "arr1", "arr2", "pm", "cm", "fin", "st", "snt"]
+
+
+def _plan(T, topo):
+    cores = list(T.cores)
+    n = len(cores)
+    rk = [topo.rack(topo.host(c)) for c in cores]
+    low = [r for r in range(n) if rk[r] == rk[0]]
+    up = [r for r in range(n) if rk[r] != rk[0]]
+    groups = {}
+    for u in up:
+        key = tuple(l for l in low if topo.may_write(cores[l], cores[u]))
+        groups.setdefault(key, []).append(u)
+    keys = sorted(groups)
+    nk = len(keys)
+    best = None
+    for m in range(2, n + 2):
+        for code in range(nk ** (m - 1)):
+            owner = [(code // nk ** p) % nk for p in range(m - 1)]
+            order, caps, used, ok = [], [], [0] * nk, True
+            for p in range(m - 1):
+                k = owner[p]
+                if used[k] >= len(keys[k]):
+                    ok = False
+                    break
+                order.append(keys[k][len(keys[k]) - 1 - used[k]])
+                caps.append(m - 1 - p)
+                used[k] += 1
+            if not ok:
+                continue
+            if any(sum(caps[p] for p in range(m - 1) if owner[p] == k) < len(groups[keys[k]]) for k in range(nk)):
+                continue
+            writes = sum(len(set(r for r in low if r > j) | set(order)) - (1 if j in order else 0) for j in low)
+            if best is None or writes < best[0]:
+                best = (writes, order, caps, owner)
+        if best is not None:
+            break
+    _, order, caps, owner = best
+    serves = {r: [] for r in order}
+    for k in range(nk):
+        left = list(groups[keys[k]])
+        mine = [p for p in range(len(order)) if owner[p] == k]
+        for p in mine:
+            same = [u for u in left if topo.chip(cores[u]) == topo.chip(cores[order[p]])]
+            if same and caps[p] > 0:
+                serves[order[p]].append(same[0])
+                left.remove(same[0])
+        for p in mine:
+            while left and len(serves[order[p]]) < caps[p]:
+                serves[order[p]].insert(0, left.pop(0))
+    order = [r for r in order if serves[r]]
+    serves = {r: serves[r] for r in order}
+    first, rest = {}, {}
+    for r in range(n):
+        grp = low if r in low else up
+        first[r] = [q for q in order if q != r] if r in low else []
+        rest[r] = [q for q in grp if q > r and q not in first[r]]
+    return {"low": low, "up": up, "serves": serves, "first": first, "rest": rest}
+
+
+def _engines(topo, src, dsts):
+    m = topo.mask(src, dsts[0])
+    for d in dsts:
+        m &= topo.mask(src, d)
+    out, cnt, bit = 0, 0, 1
+    while cnt < NE and bit <= m:
+        if m & bit:
+            out |= bit
+            cnt += 1
+        bit <<= 1
+    return out, cnt
+
+
+def _send(g, T, topo, core, ranks, src, dst, rsem):
+    dsts = [T.cores[r] for r in ranks]
+    mask, cnt = _engines(topo, core, dsts)
+    ids = []
+    for d in dsts:
+        rid, pid = topo.addr(d, core)
+        ids.append(DstId(rid=rid, pnc=pid))
+    g.remote_dma_fused([RemoteDMATransfer(dst_ids=ids, dma_engine_mask=mask, remote_sem=rsem, srcs=[src],
+                                          dsts=[dst] * len(ids), alu_op=0)], local_sem=T.sem.snt)
+    return cnt
+
+
+def rank_program(g, core, T, topo):
+    rank = T.rank_of(core)
+    if rank is None:
+        return
+    pl = _plan(T, topo)
+    S = T.sem
+    v, act, sy = g.vector, g.scalar, g.sync
+    mult, add = AluOpType.mult, AluOpType.add
+    lower = rank in pl["low"]
+    grp = pl["low"] if lower else pl["up"]
+    i = grp.index(rank)
+    relay = rank in pl["serves"]
+    calls = [c for c in (pl["first"][rank], pl["rest"][rank]) if c]
+
+    def landing(lists):
+        tot = 0
+        for s in range(len(T.cores)):
+            for lst in lists(s):
+                if rank in lst:
+                    tot += _engines(topo, T.cores[s], [T.cores[r] for r in lst])[1]
+        return tot
+    inc1 = landing(lambda s: (pl["first"][s], pl["rest"][s]))
+    inc2 = landing(lambda s: (pl["serves"].get(s, []),))
+
+    def col_a(k):
+        return T.buf[:, W:SL * (k - 1) + W + 1:SL]
+
+    def col_b(k):
+        return T.buf[:, W - 1:SL * (k - 1) + W:SL]
+
+    gate, xin, own = T.ge[:, PAD:SL], T.xe[:, PAD:SL], SL * i
+
+    sy.dma_start(T.ab[:], T.a[:]).then_inc(S.lda, 16)
+    sy.sem_inc(S.go, 1)
+    act.wait_ge(S.go, 1)
+    act.dma_start(xin, T.x[:]).then_inc(S.ldx, 16)
+    act.wait_ge(S.lda, 16)
+    act.activation(gate, T.ab[:], ActivationFunctionType.Sigmoid).then_inc(S.sg, 1)
+
+    sent = 0
+    v.wait_ge(S.sg, 1)
+    if calls or relay:
+        v.tensor_reduce(T.buf[:, own + W:own + W + 1], gate, AxisListType.X, mult).then_inc(S.sm, 1)
+    v.wait_ge(S.ldx, 16)
+    if calls or relay:
+        v.tensor_tensor_scan(T.buf[:, own:own + W], gate, xin, 0.0, mult, add).then_inc(S.sm, 1)
+        g.wait_ge(S.sm, 2)
+        pair = T.buf[:, own + W - 1:own + W + 1]
+        for lst in calls:
+            sent += _send(g, T, topo, core, lst, pair, pair, S.arr1)
+
+    if lower:
+        k = len(grp) if relay else i
+        if k:
+            if relay:
+                v.wait_ge(S.sm, 2)
+            v.wait_ge(S.arr1, inc1)
+            v.tensor_tensor_scan(T.cs[:, 0:k], col_a(k), col_b(k), 0.0, mult, add).then_inc(S.cm, 1)
+            if relay:
+                g.wait_ge(S.cm, 1)
+                sent += _send(g, T, topo, core, pl["serves"][rank], T.cs[:, k - 1:k], T.cl[:, 0:1], S.arr2)
+            v.wait_ge(S.cm, 1)
+        init, lo = (T.cs[:, i - 1:i] if i else 0.0), PAD
+    else:
+        if i:
+            v.wait_ge(S.arr1, inc1)
+            v.tensor_reduce(T.ge[:, PAD - 1:PAD], col_a(i), AxisListType.X, mult).then_inc(S.pm, 1)
+            v.tensor_tensor_scan(T.xe[:, PAD - i:PAD], col_a(i), col_b(i), 0.0, mult, add).then_inc(S.pm, 1)
+            v.wait_ge(S.pm, 2)
+        v.wait_ge(S.arr2, inc2)
+        init, lo = T.cl[:, 0:1], (PAD - 1 if i else PAD)
+
+    v.tensor_tensor_scan(T.yb[:, lo:SL], T.ge[:, lo:SL], T.xe[:, lo:SL], init, mult, add).then_inc(S.fin, 1)
+    sy.wait_ge(S.fin, 1)
+    sy.dma_start(T.y[:], T.yb[:, PAD:SL]).then_inc(S.st, 16)
+    sy.wait_ge(S.st, 16)
+    if sent:
+        g.wait_ge(S.snt, sent)

@@ -2,78 +2,25 @@ from concourse.bass import DstId, RemoteDMATransfer
 from concourse.mybir import AluOpType, AxisListType, ActivationFunctionType
 
 W = 64
-PAD = 8
-SL = PAD + W
-GROUP = 6
+RANKS = 12
+NL = 3
+ZS = 4
+LAST = ZS * (W - 1)
 NE = 8
 
 SCRATCH = {
-    "ab": ("sbuf", [128, W], "bfloat16"),
-    "xe": ("sbuf", [128, SL], "bfloat16"),
-    "ge": ("sbuf", [128, SL], "float32"),
-    "buf": ("sbuf", [128, GROUP * SL], "float32"),
-    "cs": ("sbuf", [128, 8], "float32"),
-    "cl": ("sbuf", [128, 4], "float32"),
-    "yb": ("sbuf", [128, SL], "bfloat16"),
+    "ax": ("sbuf", [128, 2 * W], "bfloat16"),
+    "rx": ("sbuf", [128, 2 * W], "bfloat16"),
+    "ge": ("sbuf", [128, W], "float32"),
+    "g2": ("sbuf", [128, W], "float32"),
+    "mb": ("sbuf", [128, ZS * W], "float32"),
+    "buf": ("sbuf", [128, ZS * RANKS], "float32"),
+    "z": ("sbuf", [128, ZS * (NL + 1 + W)], "float32"),
+    "tm": ("sbuf", [128, 16], "float32"),
+    "yb": ("sbuf", [128, W + 8], "bfloat16"),
 }
-SEMAPHORES = ["lda", "ldx", "go", "sg", "sm", "arr1", "arr2", "pm", "cm", "fin", "st", "snt"]
-
-
-def _plan(T, topo):
-    cores = list(T.cores)
-    n = len(cores)
-    rk = [topo.rack(topo.host(c)) for c in cores]
-    low = [r for r in range(n) if rk[r] == rk[0]]
-    up = [r for r in range(n) if rk[r] != rk[0]]
-    groups = {}
-    for u in up:
-        key = tuple(l for l in low if topo.may_write(cores[l], cores[u]))
-        groups.setdefault(key, []).append(u)
-    keys = sorted(groups)
-    nk = len(keys)
-    best = None
-    for m in range(2, n + 2):
-        for code in range(nk ** (m - 1)):
-            owner = [(code // nk ** p) % nk for p in range(m - 1)]
-            order, caps, used, ok = [], [], [0] * nk, True
-            for p in range(m - 1):
-                k = owner[p]
-                if used[k] >= len(keys[k]):
-                    ok = False
-                    break
-                order.append(keys[k][len(keys[k]) - 1 - used[k]])
-                caps.append(m - 1 - p)
-                used[k] += 1
-            if not ok:
-                continue
-            if any(sum(caps[p] for p in range(m - 1) if owner[p] == k) < len(groups[keys[k]]) for k in range(nk)):
-                continue
-            writes = sum(len(set(r for r in low if r > j) | set(order)) - (1 if j in order else 0) for j in low)
-            if best is None or writes < best[0]:
-                best = (writes, order, caps, owner)
-        if best is not None:
-            break
-    _, order, caps, owner = best
-    serves = {r: [] for r in order}
-    for k in range(nk):
-        left = list(groups[keys[k]])
-        mine = [p for p in range(len(order)) if owner[p] == k]
-        for p in mine:
-            same = [u for u in left if topo.chip(cores[u]) == topo.chip(cores[order[p]])]
-            if same and caps[p] > 0:
-                serves[order[p]].append(same[0])
-                left.remove(same[0])
-        for p in mine:
-            while left and len(serves[order[p]]) < caps[p]:
-                serves[order[p]].insert(0, left.pop(0))
-    order = [r for r in order if serves[r]]
-    serves = {r: serves[r] for r in order}
-    first, rest = {}, {}
-    for r in range(n):
-        grp = low if r in low else up
-        first[r] = [q for q in order if q != r] if r in low else []
-        rest[r] = [q for q in grp if q > r and q not in first[r]]
-    return {"low": low, "up": up, "serves": serves, "first": first, "rest": rest}
+SEMAPHORES = ["lda", "ldx", "raw", "sg", "sg2", "sm", "sm2", "xc", "cp", "arr1", "arr2", "pf", "pm", "pa", "cm",
+              "fin", "st", "snt"]
 
 
 def _engines(topo, src, dsts):
@@ -105,77 +52,129 @@ def rank_program(g, core, T, topo):
     rank = T.rank_of(core)
     if rank is None:
         return
-    pl = _plan(T, topo)
+    cores = list(T.cores)
+    n = len(cores)
     S = T.sem
     v, act, sy = g.vector, g.scalar, g.sync
-    mult, add = AluOpType.mult, AluOpType.add
-    lower = rank in pl["low"]
-    grp = pl["low"] if lower else pl["up"]
-    i = grp.index(rank)
-    relay = rank in pl["serves"]
-    calls = [c for c in (pl["first"][rank], pl["rest"][rank]) if c]
+    mult, add, X = AluOpType.mult, AluOpType.add, AxisListType.X
+    sigmoid = ActivationFunctionType.Sigmoid
 
-    def landing(lists):
-        tot = 0
-        for s in range(len(T.cores)):
-            for lst in lists(s):
-                if rank in lst:
-                    tot += _engines(topo, T.cores[s], [T.cores[r] for r in lst])[1]
-        return tot
-    inc1 = landing(lambda s: (pl["first"][s], pl["rest"][s]))
-    inc2 = landing(lambda s: (pl["serves"].get(s, []),))
+    def ok(s, d):
+        return topo.may_write(cores[s], cores[d])
 
-    def col_a(k):
-        return T.buf[:, W:SL * (k - 1) + W + 1:SL]
+    low = [r for r in range(n) if topo.rack(topo.host(cores[r])) == topo.rack(topo.host(cores[0]))]
+    up = [r for r in range(n) if r not in low]
+    proxy = {}
+    for l in low:
+        proxy[l] = [q for q in low if q != l and topo.same_plane(cores[l], cores[q]) and ok(l, q)
+                    and topo.chip(cores[q]) == topo.chip(cores[l])
+                    and all(ok(q, u) for u in up if not ok(l, u))][0]
+    firsts = sorted(l for l in low if l < proxy[l])
 
-    def col_b(k):
-        return T.buf[:, W - 1:SL * (k - 1) + W:SL]
+    def direct(r):
+        if r in low:
+            return [q for q in low if q > r and q != proxy[r]]
+        return [q for q in up if q > r]
 
-    gate, xin, own = T.ge[:, PAD:SL], T.xe[:, PAD:SL], SL * i
+    def served(q):
+        return [u for u in up if ok(q, u)]
 
-    sy.dma_start(T.ab[:], T.a[:]).then_inc(S.lda, 16)
-    sy.sem_inc(S.go, 1)
-    act.wait_ge(S.go, 1)
-    act.dma_start(xin, T.x[:]).then_inc(S.ldx, 16)
+    def count(src, lst):
+        return _engines(topo, cores[src], [cores[r] for r in lst])[1]
+
+    inc1 = sum(count(s, direct(s)) for s in range(n) if rank in direct(s))
+
+    def col_b(lo, k):
+        return T.buf[:, ZS * lo:ZS * (lo + k - 1) + 1:ZS]
+
+    def col_a(lo, k):
+        return T.buf[:, ZS * lo + 1:ZS * (lo + k - 1) + 2:ZS]
+
+    def slot(r):
+        return T.buf[:, ZS * r:ZS * r + 2]
+
+    def summary(lane, gates, xs, sem):
+        v.tensor_reduce(T.mb[:, LAST + lane + 1:LAST + lane + 2], gates, X, mult).then_inc(sem, 1)
+        v.tensor_tensor_scan(T.mb[:, lane:LAST + lane + 1:ZS], gates, xs, 0.0, mult, add).then_inc(sem, 1)
+
+    def made(lane):
+        return T.mb[:, LAST + lane:LAST + lane + 2]
+
+    a_in, x_in = T.ax[:, 0:W], T.ax[:, W:2 * W]
+    sy.dma_start(a_in, T.a[:]).then_inc(S.lda, 16)
+    act.dma_start(x_in, T.x[:]).then_inc(S.ldx, 16)
     act.wait_ge(S.lda, 16)
-    act.activation(gate, T.ab[:], ActivationFunctionType.Sigmoid).then_inc(S.sg, 1)
-
     sent = 0
-    v.wait_ge(S.sg, 1)
-    if calls or relay:
-        v.tensor_reduce(T.buf[:, own + W:own + W + 1], gate, AxisListType.X, mult).then_inc(S.sm, 1)
-    v.wait_ge(S.ldx, 16)
-    if calls or relay:
-        v.tensor_tensor_scan(T.buf[:, own:own + W], gate, xin, 0.0, mult, add).then_inc(S.sm, 1)
+
+    if rank in low:
+        ward = proxy[rank]
+        mine, his = (0, 2) if rank < ward else (2, 0)
+        rawinc = count(ward, [rank])
+        g.wait_ge(S.lda, 16)
+        g.wait_ge(S.ldx, 16)
+        sent += _send(g, T, topo, core, [ward], T.ax[:], T.rx[:], S.raw)
+        act.activation(T.ge[:], a_in, sigmoid).then_inc(S.sg, 1)
+        act.wait_ge(S.raw, rawinc)
+        act.activation(T.g2[:], T.rx[:, 0:W], sigmoid).then_inc(S.sg2, 1)
+        v.wait_ge(S.sg, 1)
+        v.wait_ge(S.ldx, 16)
+        summary(mine, T.ge[:], x_in, S.sm)
         g.wait_ge(S.sm, 2)
-        pair = T.buf[:, own + W - 1:own + W + 1]
-        for lst in calls:
-            sent += _send(g, T, topo, core, lst, pair, pair, S.arr1)
-
-    if lower:
-        k = len(grp) if relay else i
-        if k:
-            if relay:
-                v.wait_ge(S.sm, 2)
-            v.wait_ge(S.arr1, inc1)
-            v.tensor_tensor_scan(T.cs[:, 0:k], col_a(k), col_b(k), 0.0, mult, add).then_inc(S.cm, 1)
-            if relay:
-                g.wait_ge(S.cm, 1)
-                sent += _send(g, T, topo, core, pl["serves"][rank], T.cs[:, k - 1:k], T.cl[:, 0:1], S.arr2)
+        if direct(rank):
+            sent += _send(g, T, topo, core, direct(rank), made(mine), slot(rank), S.arr1)
+        v.wait_ge(S.sg2, 1)
+        v.wait_ge(S.raw, rawinc)
+        summary(his, T.g2[:], T.rx[:, W:2 * W], S.sm2)
+        g.wait_ge(S.sm2, 2)
+        s = firsts.index(min(rank, ward))
+        sent += _send(g, T, topo, core, served(rank), T.mb[:, LAST:LAST + ZS], T.z[:, ZS * s:ZS * s + ZS], S.arr2)
+        init = 0.0
+        if rank:
+            if ward < rank:
+                v.wait_ge(S.sm2, 2)
+                v.tensor_copy(slot(ward), made(his)).then_inc(S.cp, 1)
+                v.wait_ge(S.cp, 1)
+            if inc1:
+                v.wait_ge(S.arr1, inc1)
+            v.tensor_tensor_scan(T.tm[:, 0:rank], col_a(0, rank), col_b(0, rank), 0.0, mult, add).then_inc(S.cm, 1)
             v.wait_ge(S.cm, 1)
-        init, lo = (T.cs[:, i - 1:i] if i else 0.0), PAD
+            init = T.tm[:, rank - 1:rank]
+        v.tensor_tensor_scan(T.yb[:, 0:W], T.ge[:], x_in, init, mult, add).then_inc(S.fin, 1)
+        y_sb = T.yb[:, 0:W]
     else:
-        if i:
+        k = rank - up[0]
+        f = 1 if k else 0
+        ow = ZS * (NL + f)
+        zx = T.z[:, ow + 2:ow + LAST + 3:ZS]
+        zg = T.z[:, ow + 3:ow + LAST + 4:ZS]
+        act.activation(zg, a_in, sigmoid).then_inc(S.sg, 1)
+        v.wait_ge(S.ldx, 16)
+        v.tensor_copy(zx, x_in).then_inc(S.xc, 1)
+        v.wait_ge(S.sg, 1)
+        v.wait_ge(S.xc, 1)
+        if direct(rank):
+            summary(0, zg, zx, S.sm)
+            g.wait_ge(S.sm, 2)
+            sent += _send(g, T, topo, core, direct(rank), made(0), slot(rank), S.arr1)
+        if k:
             v.wait_ge(S.arr1, inc1)
-            v.tensor_reduce(T.ge[:, PAD - 1:PAD], col_a(i), AxisListType.X, mult).then_inc(S.pm, 1)
-            v.tensor_tensor_scan(T.xe[:, PAD - i:PAD], col_a(i), col_b(i), 0.0, mult, add).then_inc(S.pm, 1)
+            v.tensor_reduce(T.z[:, ZS * NL + 3:ZS * NL + 4], col_a(up[0], k), X, mult).then_inc(S.pm, 1)
+            v.tensor_tensor_scan(T.tm[:, 0:k], col_a(up[0], k), col_b(up[0], k), 0.0, mult, add).then_inc(S.pf, 1)
+            v.wait_ge(S.pf, 1)
+            v.tensor_copy(T.z[:, ZS * NL + 2:ZS * NL + 3], T.tm[:, k - 1:k]).then_inc(S.pm, 1)
             v.wait_ge(S.pm, 2)
+        inc2 = sum(count(q, served(q)) for q in low if rank in served(q))
         v.wait_ge(S.arr2, inc2)
-        init, lo = T.cl[:, 0:1], (PAD - 1 if i else PAD)
+        v.tensor_tensor_scan(T.tm[:, 8:8 + NL], T.z[:, 1:ZS * (NL - 1) + 2:ZS], T.z[:, 0:ZS * (NL - 1) + 1:ZS], 0.0,
+                             mult, add).then_inc(S.pa, 1)
+        v.wait_ge(S.pa, 1)
+        m = NL + f + W
+        v.tensor_tensor_scan(T.yb[:, 0:m], T.z[:, 3:ZS * (m - 1) + 4:ZS], T.z[:, 2:ZS * (m - 1) + 3:ZS],
+                             T.tm[:, 8 + NL - 1:8 + NL], mult, add).then_inc(S.fin, 1)
+        y_sb = T.yb[:, NL + f:m]
 
-    v.tensor_tensor_scan(T.yb[:, lo:SL], T.ge[:, lo:SL], T.xe[:, lo:SL], init, mult, add).then_inc(S.fin, 1)
     sy.wait_ge(S.fin, 1)
-    sy.dma_start(T.y[:], T.yb[:, PAD:SL]).then_inc(S.st, 16)
+    sy.dma_start(T.y[:], y_sb).then_inc(S.st, 16)
     sy.wait_ge(S.st, 16)
     if sent:
         g.wait_ge(S.snt, sent)

from concourse.bass import DstId, RemoteDMATransfer
from concourse.mybir import AluOpType, AxisListType, ActivationFunctionType

W = 64
RANKS = 12
NL = 3
ZS = 4
LAST = ZS * (W - 1)
NE = 8

SCRATCH = {
    "ax": ("sbuf", [128, 2 * W], "bfloat16"),
    "rx": ("sbuf", [128, 2 * W], "bfloat16"),
    "ge": ("sbuf", [128, W], "float32"),
    "g2": ("sbuf", [128, W], "float32"),
    "mb": ("sbuf", [128, ZS * W], "float32"),
    "buf": ("sbuf", [128, ZS * RANKS], "float32"),
    "z": ("sbuf", [128, ZS * (NL + 1 + W)], "float32"),
    "tm": ("sbuf", [128, 16], "float32"),
    "yb": ("sbuf", [128, W + 8], "bfloat16"),
}
SEMAPHORES = ["lda", "ldx", "raw", "sg", "sg2", "sm", "sm2", "xc", "cp", "arr1", "arr2", "pf", "pm", "pa", "cm",
              "fin", "st", "snt"]


def _engines(topo, src, dsts):
    m = topo.mask(src, dsts[0])
    for d in dsts:
        m &= topo.mask(src, d)
    out, cnt, bit = 0, 0, 1
    while cnt < NE and bit <= m:
        if m & bit:
            out |= bit
            cnt += 1
        bit <<= 1
    return out, cnt


def _send(g, T, topo, core, ranks, src, dst, rsem):
    dsts = [T.cores[r] for r in ranks]
    mask, cnt = _engines(topo, core, dsts)
    ids = []
    for d in dsts:
        rid, pid = topo.addr(d, core)
        ids.append(DstId(rid=rid, pnc=pid))
    g.remote_dma_fused([RemoteDMATransfer(dst_ids=ids, dma_engine_mask=mask, remote_sem=rsem, srcs=[src],
                                          dsts=[dst] * len(ids), alu_op=0)], local_sem=T.sem.snt)
    return cnt


def rank_program(g, core, T, topo):
    rank = T.rank_of(core)
    if rank is None:
        return
    cores = list(T.cores)
    n = len(cores)
    S = T.sem
    v, act, sy = g.vector, g.scalar, g.sync
    mult, add, X = AluOpType.mult, AluOpType.add, AxisListType.X
    sigmoid = ActivationFunctionType.Sigmoid

    def ok(s, d):
        return topo.may_write(cores[s], cores[d])

    low = [r for r in range(n) if topo.rack(topo.host(cores[r])) == topo.rack(topo.host(cores[0]))]
    up = [r for r in range(n) if r not in low]
    proxy = {}
    for l in low:
        proxy[l] = [q for q in low if q != l and topo.same_plane(cores[l], cores[q]) and ok(l, q)
                    and topo.chip(cores[q]) == topo.chip(cores[l])
                    and all(ok(q, u) for u in up if not ok(l, u))][0]
    firsts = sorted(l for l in low if l < proxy[l])

    def direct(r):
        if r in low:
            return [q for q in low if q > r and q != proxy[r]]
        return [q for q in up if q > r]

    def served(q):
        return [u for u in up if ok(q, u)]

    def count(src, lst):
        return _engines(topo, cores[src], [cores[r] for r in lst])[1]

    inc1 = sum(count(s, direct(s)) for s in range(n) if rank in direct(s))

    def col_b(lo, k):
        return T.buf[:, ZS * lo:ZS * (lo + k - 1) + 1:ZS]

    def col_a(lo, k):
        return T.buf[:, ZS * lo + 1:ZS * (lo + k - 1) + 2:ZS]

    def slot(r):
        return T.buf[:, ZS * r:ZS * r + 2]

    def summary(lane, gates, xs, sem):
        v.tensor_reduce(T.mb[:, LAST + lane + 1:LAST + lane + 2], gates, X, mult).then_inc(sem, 1)
        v.tensor_tensor_scan(T.mb[:, lane:LAST + lane + 1:ZS], gates, xs, 0.0, mult, add).then_inc(sem, 1)

    def made(lane):
        return T.mb[:, LAST + lane:LAST + lane + 2]

    a_in, x_in = T.ax[:, 0:W], T.ax[:, W:2 * W]
    sy.dma_start(a_in, T.a[:]).then_inc(S.lda, 16)
    act.dma_start(x_in, T.x[:]).then_inc(S.ldx, 16)
    act.wait_ge(S.lda, 16)
    sent = 0

    if rank in low:
        ward = proxy[rank]
        mine, his = (0, 2) if rank < ward else (2, 0)
        rawinc = count(ward, [rank])
        g.wait_ge(S.lda, 16)
        g.wait_ge(S.ldx, 16)
        sent += _send(g, T, topo, core, [ward], T.ax[:], T.rx[:], S.raw)
        act.activation(T.ge[:], a_in, sigmoid).then_inc(S.sg, 1)
        act.wait_ge(S.raw, rawinc)
        act.activation(T.g2[:], T.rx[:, 0:W], sigmoid).then_inc(S.sg2, 1)
        v.wait_ge(S.sg, 1)
        v.wait_ge(S.ldx, 16)
        summary(mine, T.ge[:], x_in, S.sm)
        g.wait_ge(S.sm, 2)
        if direct(rank):
            sent += _send(g, T, topo, core, direct(rank), made(mine), slot(rank), S.arr1)
        v.wait_ge(S.sg2, 1)
        v.wait_ge(S.raw, rawinc)
        summary(his, T.g2[:], T.rx[:, W:2 * W], S.sm2)
        g.wait_ge(S.sm2, 2)
        s = firsts.index(min(rank, ward))
        sent += _send(g, T, topo, core, served(rank), T.mb[:, LAST:LAST + ZS], T.z[:, ZS * s:ZS * s + ZS], S.arr2)
        init = 0.0
        if rank:
            if ward < rank:
                v.wait_ge(S.sm2, 2)
                v.tensor_copy(slot(ward), made(his)).then_inc(S.cp, 1)
                v.wait_ge(S.cp, 1)
            if inc1:
                v.wait_ge(S.arr1, inc1)
            v.tensor_tensor_scan(T.tm[:, 0:rank], col_a(0, rank), col_b(0, rank), 0.0, mult, add).then_inc(S.cm, 1)
            v.wait_ge(S.cm, 1)
            init = T.tm[:, rank - 1:rank]
        v.tensor_tensor_scan(T.yb[:, 0:W], T.ge[:], x_in, init, mult, add).then_inc(S.fin, 1)
        y_sb = T.yb[:, 0:W]
    else:
        k = rank - up[0]
        f = 1 if k else 0
        ow = ZS * (NL + f)
        zx = T.z[:, ow + 2:ow + LAST + 3:ZS]
        zg = T.z[:, ow + 3:ow + LAST + 4:ZS]
        act.activation(zg, a_in, sigmoid).then_inc(S.sg, 1)
        v.wait_ge(S.ldx, 16)
        v.tensor_copy(zx, x_in).then_inc(S.xc, 1)
        v.wait_ge(S.sg, 1)
        v.wait_ge(S.xc, 1)
        if direct(rank):
            summary(0, zg, zx, S.sm)
            g.wait_ge(S.sm, 2)
            sent += _send(g, T, topo, core, direct(rank), made(0), slot(rank), S.arr1)
        if k:
            v.wait_ge(S.arr1, inc1)
            v.tensor_reduce(T.z[:, ZS * NL + 3:ZS * NL + 4], col_a(up[0], k), X, mult).then_inc(S.pm, 1)
            v.tensor_tensor_scan(T.tm[:, 0:k], col_a(up[0], k), col_b(up[0], k), 0.0, mult, add).then_inc(S.pf, 1)
            v.wait_ge(S.pf, 1)
            v.tensor_copy(T.z[:, ZS * NL + 2:ZS * NL + 3], T.tm[:, k - 1:k]).then_inc(S.pm, 1)
            v.wait_ge(S.pm, 2)
        inc2 = sum(count(q, served(q)) for q in low if rank in served(q))
        v.wait_ge(S.arr2, inc2)
        v.tensor_tensor_scan(T.tm[:, 8:8 + NL], T.z[:, 1:ZS * (NL - 1) + 2:ZS], T.z[:, 0:ZS * (NL - 1) + 1:ZS], 0.0,
                             mult, add).then_inc(S.pa, 1)
        v.wait_ge(S.pa, 1)
        m = NL + f + W
        v.tensor_tensor_scan(T.yb[:, 0:m], T.z[:, 3:ZS * (m - 1) + 4:ZS], T.z[:, 2:ZS * (m - 1) + 3:ZS],
                             T.tm[:, 8 + NL - 1:8 + NL], mult, add).then_inc(S.fin, 1)
        y_sb = T.yb[:, NL + f:m]

    sy.wait_ge(S.fin, 1)
    sy.dma_start(T.y[:], y_sb).then_inc(S.st, 16)
    sy.wait_ge(S.st, 16)
    if sent:
        g.wait_ge(S.snt, sent)
